import numpy as np
import ml_dtypes


def mxq(x, axis, fmt="e4m3"):
    dtype, down = {"e4m3": (ml_dtypes.float8_e4m3fn, 7), "e5m2": (ml_dtypes.float8_e5m2, 14)}[fmt]
    v = np.moveaxis(np.asarray(x, np.float32).astype(ml_dtypes.bfloat16).astype(np.float64), axis, -1)
    blocks = v.reshape(v.shape[:-1] + (-1, 32))
    amax = np.abs(blocks).max(-1, keepdims=True)
    byte = np.maximum(np.where(amax > 0, np.frexp(amax)[1] - 1 + 127, 0) - down, 1)
    scale = np.exp2(byte - 127.0)
    codes = (blocks / scale).astype(np.float32).astype(dtype).astype(np.float64)
    return np.moveaxis((codes * scale).reshape(v.shape), -1, axis)


WIDE = False


def mx_kscale(k):
    if not WIDE:
        return np.ones(k)
    levels = np.array([10, -10, 5, -5, 0])
    if k % 512:
        return np.exp2(np.random.permutation(np.resize(levels, k // 32))).repeat(32)
    a = np.empty((k // 512, 16))
    for p in range(k // 512):
        a[p, :8] = np.random.permutation(np.resize(levels, 8))
        for g in range(8):
            far = levels[np.abs(levels - a[p, g]) >= 10]
            a[p, g + 8] = far[np.random.randint(len(far))]
    return np.exp2(a.ravel()).repeat(32)


def f64(x):
    return np.asarray(x).astype(np.float64)


def striped(idx):
    return np.tile(idx.reshape(-1, 16).T, (8, 1)).astype(np.uint16)


def unstriped(offs):
    return offs[:16].T.reshape(-1).astype(np.int64)


def pack_weight(w):
    k, n = w.shape
    w = f64(np.asarray(w, np.float32).astype(ml_dtypes.bfloat16)).reshape(k // 32, 32, n)
    amax = np.abs(w).max(1)
    byte = np.clip(np.where(amax > 0, np.frexp(amax)[1] - 1 + 127 - 7, 1), 1, 254)
    scaled = (w * np.exp2(127.0 - byte)[:, None, :]).reshape(k, n).astype(np.float32)
    words = np.ascontiguousarray(scaled.reshape(k // 512, 128, 4, n).transpose(0, 1, 3, 2)).astype(ml_dtypes.float8_e4m3fn).view(np.uint8)
    return words, np.ascontiguousarray(byte.astype(np.uint8).reshape(k // 512, 16, n))


def unpack_weight(words, scales):
    g, p, n, _ = words.shape
    vals = np.ascontiguousarray(words).view(ml_dtypes.float8_e4m3fn).astype(np.float64) * np.repeat(np.exp2(scales.astype(np.float64) - 127.0), 8, axis=1)[..., None]
    return vals.transpose(0, 1, 3, 2).reshape(g * 512, n)


E2M1 = np.array([0.0, 0.5, 1.0, 1.5, 2.0, 3.0, 4.0, 6.0, -0.0, -0.5, -1.0, -1.5, -2.0, -3.0, -4.0, -6.0])


def pack_fp4(w):
    k, n = w.shape
    w = f64(np.asarray(w, np.float32).astype(ml_dtypes.bfloat16)).reshape(k // 32, 32, n)
    amax = np.abs(w).max(1)
    mant, ex = np.frexp(amax / 6.0)
    byte = np.clip(np.where(amax > 0, np.where(mant > 0.5, ex, ex - 1) + 127, 1), 1, 254)
    scaled = (w * np.exp2(127.0 - byte)[:, None, :]).reshape(k, n).astype(np.float32)
    c = np.ascontiguousarray(scaled.reshape(k // 512, 128, 4, n).transpose(0, 1, 3, 2)).astype(ml_dtypes.float4_e2m1fn).view(np.uint8) & 0xF
    words = (c[..., 0::2] | (c[..., 1::2] << 4)).reshape(k // 512, 128, 2 * n)
    return np.ascontiguousarray(words), np.ascontiguousarray(byte.astype(np.uint8).reshape(k // 512, 16, n))


def unpack_fp4(words, scales):
    g, _, n = scales.shape
    words = np.ascontiguousarray(words).reshape(g, 128, n, 2)
    nib = np.empty((g, 128, n, 4), np.uint8)
    nib[..., 0::2] = words & 0xF
    nib[..., 1::2] = words >> 4
    vals = E2M1[nib] * np.repeat(np.exp2(scales.astype(np.float64) - 127.0), 8, axis=1)[..., None]
    return vals.transpose(0, 1, 3, 2).reshape(g * 512, n)


def planes(y):
    n, m = y.shape
    v = y.astype(np.float32).astype(ml_dtypes.bfloat16).astype(np.float64).reshape(n // 32, 32, m)
    top = np.abs(v).max(1)
    byte = np.clip(np.where(top > 0, np.frexp(top)[1] - 1 + 127 - 7, 1), 1, 254)
    codes = (v * np.exp2(127.0 - byte)[:, None, :]).reshape(n, m).astype(np.float32).astype(ml_dtypes.float8_e4m3fn).view(np.uint8)
    words = codes.reshape(n // 512, 128, 4, m).transpose(0, 1, 3, 2)
    return np.ascontiguousarray(words), np.ascontiguousarray(byte.astype(np.uint8).reshape(n // 512, 16, m))


K, T, S, N, H, U = 512, 2048, 512, 512, 512, 1024


def setup_inputs():
    n = np.random.standard_normal
    s = mx_kscale(K)[:, None]
    u = mx_kscale(H)
    packed_xT = pack_weight(n((K, T)) * s)
    packed_w1 = pack_fp4(n((K, N)) / np.sqrt(K) / s)
    packed_w2 = pack_fp4(n((K, N)) / np.sqrt(K) / s)
    packed_w3 = pack_fp4(n((H, N)) / np.sqrt(H) / u[:, None])
    return {
        "x_words": packed_xT[0],
        "x_scales": packed_xT[1],
        "w1_words": packed_w1[0],
        "w1_scales": packed_w1[1],
        "w2_words": packed_w2[0],
        "w2_scales": packed_w2[1],
        "unit": (np.random.uniform(0.6, 1.4, (H, 1)) * u[:, None]).astype(np.float32),
        "w3_words": packed_w3[0],
        "w3_scales": packed_w3[1],
        "offs": striped(np.random.permutation(T)[:S]),
        "use": striped(np.random.permutation(np.concatenate([np.arange(S), np.random.randint(0, S, U - S)]))),
        "alt1": striped(np.random.permutation(np.concatenate([np.arange(S), np.random.randint(0, S, U - S)]))),
        "alt2": striped(np.random.permutation(np.concatenate([np.arange(S), np.random.randint(0, S, U - S)]))),
    }


def reference(x_words, x_scales, w1_words, w1_scales, w2_words, w2_scales, unit, w3_words, w3_scales, offs, use, alt1, alt2):
    xq = unpack_weight(x_words, x_scales)[:, unstriped(offs)]
    y = unpack_fp4(w1_words, w1_scales).T @ xq
    yu = y[:, unstriped(use)]
    y_1 = y[:, unstriped(alt1)]
    z1 = unpack_fp4(w2_words, w2_scales).T @ xq
    z_2 = z1[:, unstriped(alt2)]
    hid = f64(unit) * (np.maximum(yu, y_1) * z_2)
    out_0 = unpack_fp4(w3_words, w3_scales).T @ mxq(hid, 0, "e4m3")
    return (out_0,) + planes(out_0)

@@ -1,0 +1,196 @@
+from contextlib import ExitStack
+
+import concourse.mybir as mybir
+
+F32 = mybir.dt.float32
+BF16 = mybir.dt.bfloat16
+I32 = mybir.dt.int32
+U32 = mybir.dt.uint32
+U16 = mybir.dt.uint16
+U8 = mybir.dt.uint8
+FP8X4 = mybir.dt.float8_e4m3fn_x4
+FP4X4 = mybir.dt.float4_e2m1fn_x4
+ALU = mybir.AluOpType
+COPY = mybir.ActivationFunctionType.Copy
+
+P = 128
+PACK = 4
+T, S, U = 2048, 512, 1024
+FLOPS = 2 * 512 * 512 * (S + S + U)
+CHUNKS = [384, 256, 256, 128]
+SPARE = 16
+ROUND_ON_SCALAR = []
+DEAL = "SVV"
+RING = 3
+BEST = 3
+LAG = 1
+AFTER = [1, 2, 3, 5, 6]
+Y_ON_SCALAR = 1
+BANK = 512
+
+
+def tile_picked_ytoolrt_gate_po_kernel(tc, x_words, x_scales, w1_words, w1_scales, w2_words, w2_scales, unit, w3_words, w3_scales, offs, use, alt1, alt2, out_0, out_1, out_2):
+    nc = tc.nc
+    with ExitStack() as ctx:
+        keep = ctx.enter_context(tc.tile_pool(name="keep", bufs=1))
+        psum = ctx.enter_context(tc.psum_pool(name="psum", bufs=8))
+
+        def scale_rows(queues, plane, scales):
+            for q in range(4):
+                queues[q].dma_start(plane[32 * q : 32 * q + 4, :].bitcast(I32), scales[0, 4 * q : 4 * q + 4, :].bitcast(I32))
+
+        offs_t = keep.tile([P, S // 16], U16, name="offs_t")
+        use_t = keep.tile([P, U // 16], U16, name="use_t")
+        alt1_t = keep.tile([P, U // 16], U16, name="alt1_t")
+        alt2_t = keep.tile([P, U // 16], U16, name="alt2_t")
+        x_table = keep.tile([P, T], I32, name="x_table", align_bytes=64)
+        x_plane = keep.tile([P, T], U8, name="x_plane", align_bytes=64)
+        unit_t = keep.tile([P, PACK], F32, name="unit_t")
+        raw_words = [keep.tile([P, 2 * S], U8, name=f"raw_words{w}", align_bytes=64) for w in range(3)]
+        raw_plane = [keep.tile([P, S], U8, name=f"raw_plane{w}", align_bytes=64) for w in range(3)]
+        w_words = [keep.tile([P, 2 * S], U8, name=f"w_words{w}", align_bytes=64) for w in range(3)]
+        w_plane = [keep.tile([P, S], U8, name=f"w_plane{w}", align_bytes=64) for w in range(3)]
+
+        nc.vector.memset(x_plane[:].bitcast(I32), 0)
+        nc.vector.memset(raw_plane[0][:].bitcast(I32), 0)
+        nc.vector.memset(raw_plane[1][:].bitcast(I32), 0)
+        nc.vector.memset(raw_plane[2][:].bitcast(I32), 0)
+
+        nc.sync.dma_start(offs_t[:], offs)
+        nc.scalar.dma_start(x_table[:], x_words[0].rearrange("p c r -> p (c r)").bitcast(I32))
+        nc.sync.dma_start(raw_words[0][:].bitcast(I32), w1_words[0].bitcast(I32))
+        scale_rows([nc.sync] * 4, x_plane, x_scales)
+        scale_rows([nc.sync] * 4, raw_plane[0], w1_scales)
+        nc.sync.dma_start(use_t[:], use)
+        nc.sync.dma_start(alt1_t[:], alt1)
+        nc.sync.dma_start(raw_words[1][:].bitcast(I32), w2_words[0].bitcast(I32))
+        scale_rows([nc.sync] * 4, raw_plane[1], w2_scales)
+        nc.gpsimd.dma_start(unit_t[:], unit.rearrange("(p t) o -> p (t o)", t=PACK))
+        nc.sync.dma_start(alt2_t[:], alt2)
+        nc.sync.dma_start(raw_words[2][:].bitcast(I32), w3_words[0].bitcast(I32))
+        scale_rows([nc.sync] * 4, raw_plane[2], w3_scales)
+
+        def deal_words(w):
+            if DEAL[w] == "V":
+                nc.vector.tensor_copy(w_words[w][:].rearrange("p (t m b) -> p t m b", t=PACK, b=2), raw_words[w][:].rearrange("p (m t b) -> p t m b", t=PACK, b=2))
+            else:
+                nc.scalar.copy(w_words[w][:].bitcast(U16).rearrange("p (t m) -> p t m", t=PACK), raw_words[w][:].bitcast(U16).rearrange("p (m t) -> p t m", t=PACK))
+
+        def deal_plane(w):
+            nc.vector.tensor_copy(w_plane[w][:].rearrange("p (t m) -> p t m", t=PACK), raw_plane[w][:].rearrange("p (m t) -> p t m", t=PACK))
+
+        def product(acc, w, t, codes, plane):
+            nc.tensor.matmul_mx(out=acc, lhsT=w_words[w][:, 2 * P * t : 2 * P * (t + 1)].bitcast(FP4X4), lhsT_scale=w_plane[w][:, P * t : P * (t + 1)],
+                                rhs=codes.bitcast(FP8X4), rhs_scale=plane, start=True, stop=True)
+
+        xq_words = keep.tile([P, S], U32, name="xq_words", align_bytes=64)
+        xq_plane = keep.tile([P, S], U8, name="xq_plane", align_bytes=64)
+        deal_words(0)
+        nc.vector.tensor_copy(xq_plane[:], x_plane[:].indirect(offs_t[:]))
+        deal_plane(0)
+        nc.vector.tensor_copy(xq_words[:], x_table[:].bitcast(U32).indirect(offs_t[:]))
+        deal_words(1)
+        deal_plane(1)
+
+        spare = SPARE if max(CHUNKS) == S else 0
+        y = [keep.tile([P, S + spare], F32, name=f"y{t}") for t in range(PACK)]
+        z = [keep.tile([P, S + spare], F32, name=f"z{t}") for t in range(PACK)]
+        for window in y + z:
+            if spare:
+                nc.gpsimd.memset(window[:, S:], 0.0)
+        y_banks = []
+        for t in range(PACK):
+            acc = psum.tile([P, BANK], F32, name="acc")
+            product(acc[:], 0, t, xq_words[:], xq_plane[:])
+            y_banks.append(acc)
+            if t >= Y_ON_SCALAR:
+                nc.vector.tensor_copy(y[t][:, :S], acc[:])
+            acc = psum.tile([P, BANK], F32, name="acc")
+            product(acc[:], 1, t, xq_words[:], xq_plane[:])
+            nc.vector.tensor_scalar(z[t][:, :S], acc[:], unit_t[:, t : t + 1], None, ALU.mult)
+        deal_words(2)
+        deal_plane(2)
+
+        out_codes = keep.tile([P, U], U32, name="out_codes", align_bytes=64)
+        out_plane = keep.tile([P, U], U8, name="out_plane", align_bytes=64)
+        out_rows = out_0.rearrange("(p t) r -> p t r", t=PACK)
+        out_words = out_1[0].rearrange("p c r -> p (c r)").bitcast(I32)
+
+        def interleave(dst, src, on_scalar=False):
+            (nc.scalar.copy if on_scalar else nc.vector.tensor_copy)(dst.rearrange("p (c i t) -> p c t i", i=4, t=PACK), src.rearrange("p t (c i) -> p c t i", i=4))
+
+        starts = [sum(CHUNKS[:c]) for c in range(len(CHUNKS))]
+
+        def larger(c, t):
+            c0, n = starts[c], CHUNKS[c]
+            lists = slice(c0 // 16, (c0 + n) // 16)
+            used = keep.tile([P, n], F32, name="used", bufs=RING)
+            other = keep.tile([P, n], F32, name="other", bufs=RING)
+            best = keep.tile([P, n], F32, name="best", bufs=BEST)
+            nc.scalar.activation(used[:], y[t][:].indirect(use_t[:, lists]), COPY)
+            nc.scalar.activation(other[:], y[t][:].indirect(alt1_t[:, lists]), COPY)
+            nc.vector.tensor_tensor(best[:], used[:], other[:], ALU.max)
+            return best
+
+        def gate(hid, c, t, best):
+            c0, n = starts[c], CHUNKS[c]
+            lists = slice(c0 // 16, (c0 + n) // 16)
+            nc.vector.tensor_tensor(hid[:, t, :], z[t][:].indirect(alt2_t[:, lists]), best[:], ALU.mult)
+
+        def round_hid(c):
+            n = CHUNKS[c]
+            hid16[c] = keep.tile([P, PACK * n], BF16, name=f"hid16_{c}", align_bytes=64)
+            interleave(hid16[c][:], hid[c][:])
+
+        def last_product(c):
+            n = CHUNKS[c]
+            codes = keep.tile([P, n], U32, name="codes", tag=f"codes{c}", align_bytes=64)
+            plane = keep.tile([P, n], U8, name=f"plane_{c}", align_bytes=64)
+            nc.vector.quantize_mx(out=codes[:].bitcast(FP8X4), scales=plane[:], in_=hid16[c][:])
+            banks[c] = [psum.tile([P, BANK], F32, name="acc") for b in range(PACK * n // BANK)]
+            for t in range(PACK):
+                j = 0
+                while j < n:
+                    b, at = divmod(t * n + j, BANK)
+                    width = max(w for w in (128, 256, 512) if w <= min(n - j, BANK - at))
+                    product(banks[c][b][:, at : at + width], 2, t, codes[:, j : j + width], plane[:, j : j + width])
+                    j += width
+
+        def leave_psum(c):
+            c0, n = starts[c], CHUNKS[c]
+            res[c] = keep.tile([P, PACK, n], F32, name=f"res_{c}")
+            flat = res[c][:].rearrange("p t n -> p (t n)")
+            for b, acc in enumerate(banks[c]):
+                nc.scalar.copy(flat[:, b * BANK : (b + 1) * BANK], acc[:])
+            nc.sync.dma_start(out_rows[:, :, c0 : c0 + n], res[c][:])
+
+        def round_out(c):
+            res16[c] = keep.tile([P, PACK * CHUNKS[c]], BF16, name=f"res16_{c}", align_bytes=64)
+            interleave(res16[c][:], res[c][:], c in ROUND_ON_SCALAR)
+
+        def hand_on(c):
+            c0, n = starts[c], CHUNKS[c]
+            nc.vector.quantize_mx(out=out_codes[:, c0 : c0 + n].bitcast(FP8X4), scales=out_plane[:, c0 : c0 + n], in_=res16[c][:])
+            nc.sync.dma_start(out_words[:, c0 : c0 + n], out_codes[:, c0 : c0 + n].bitcast(I32))
+
+        hid, hid16, banks, res, res16, best = {}, {}, {}, {}, {}, {}
+        stages = [round_hid, last_product, leave_psum, round_out, hand_on]
+        steps = PACK * len(CHUNKS)
+        for step in range(steps + LAG + max(AFTER)):
+            c, t = divmod(step, PACK)
+            for stage, after in zip(stages, AFTER):
+                done, rest = divmod(step - LAG - after - (PACK - 1), PACK)
+                if rest == 0 and 0 <= done < len(CHUNKS):
+                    stage(done)
+            if step < steps:
+                if step < Y_ON_SCALAR:
+                    nc.scalar.copy(y[t][:, :S], y_banks[t][:])
+                if t == 0:
+                    hid[c] = keep.tile([P, PACK, CHUNKS[c]], F32, name=f"hid_{c}")
+                best[step] = larger(c, t)
+            if 0 <= step - LAG < steps:
+                c, t = divmod(step - LAG, PACK)
+                gate(hid[c], c, t, best[step - LAG])
+        for q in range(4):
+            queue = nc.sync if q % 2 else nc.scalar
+            queue.dma_start(out_2[0, 4 * q : 4 * q + 4, :].bitcast(I32), out_plane[32 * q : 32 * q + 4, :].bitcast(I32))

@@ -17,13 +17,17 @@ P = 128
 PACK = 4
 T, S, U = 2048, 512, 1024
 FLOPS = 2 * 512 * 512 * (S + S + U)
-CHUNKS = [384, 256, 256, 128]
+CHUNKS = [512, 384, 128]
 SPARE = 16
+HOLD = True
+THIRD = 2
+CHAIN = True
 ROUND_ON_SCALAR = []
-DEAL = "SVV"
+DEAL = "SSV"
 RING = 3
-BEST = 3
-LAG = 1
+BEST = 2
+PAIR = 4
+Z_ON_SCALAR = [(1, 3), (2, 3), (2, 2)]
 AFTER = [1, 2, 3, 5, 6]
 Y_ON_SCALAR = 1
 BANK = 512
@@ -35,9 +39,9 @@ def tile_picked_ytoolrt_gate_po_kernel(tc, x_words, x_scales, w1_words, w1_scale
         keep = ctx.enter_context(tc.tile_pool(name="keep", bufs=1))
         psum = ctx.enter_context(tc.psum_pool(name="psum", bufs=8))
 
-        def scale_rows(queues, plane, scales):
-            for q in range(4):
-                queues[q].dma_start(plane[32 * q : 32 * q + 4, :].bitcast(I32), scales[0, 4 * q : 4 * q + 4, :].bitcast(I32))
+        def scale_rows(plane, scales, quadrants):
+            for q in quadrants:
+                nc.sync.dma_start(plane[32 * q : 32 * q + 4, :].bitcast(I32), scales[0, 4 * q : 4 * q + 4, :].bitcast(I32))
 
         offs_t = keep.tile([P, S // 16], U16, name="offs_t")
         use_t = keep.tile([P, U // 16], U16, name="use_t")
@@ -48,8 +52,7 @@ def tile_picked_ytoolrt_gate_po_kernel(tc, x_words, x_scales, w1_words, w1_scale
         unit_t = keep.tile([P, PACK], F32, name="unit_t")
         raw_words = [keep.tile([P, 2 * S], U8, name=f"raw_words{w}", align_bytes=64) for w in range(3)]
         raw_plane = [keep.tile([P, S], U8, name=f"raw_plane{w}", align_bytes=64) for w in range(3)]
-        w_words = [keep.tile([P, 2 * S], U8, name=f"w_words{w}", align_bytes=64) for w in range(3)]
-        w_plane = [keep.tile([P, S], U8, name=f"w_plane{w}", align_bytes=64) for w in range(3)]
+        w_words, w_plane = {}, {}
 
         nc.vector.memset(x_plane[:].bitcast(I32), 0)
         nc.vector.memset(raw_plane[0][:].bitcast(I32), 0)
@@ -57,26 +60,29 @@ def tile_picked_ytoolrt_gate_po_kernel(tc, x_words, x_scales, w1_words, w1_scale
         nc.vector.memset(raw_plane[2][:].bitcast(I32), 0)
 
         nc.sync.dma_start(offs_t[:], offs)
-        nc.scalar.dma_start(x_table[:], x_words[0].rearrange("p c r -> p (c r)").bitcast(I32))
         nc.sync.dma_start(raw_words[0][:].bitcast(I32), w1_words[0].bitcast(I32))
-        scale_rows([nc.sync] * 4, x_plane, x_scales)
-        scale_rows([nc.sync] * 4, raw_plane[0], w1_scales)
+        nc.gpsimd.dma_start(raw_words[1][:].bitcast(I32), w2_words[0].bitcast(I32))
+        nc.gpsimd.dma_start(unit_t[:], unit.rearrange("(p t) o -> p (t o)", t=PACK))
+        scale_rows(x_plane, x_scales, range(4))
+        scale_rows(raw_plane[0], w1_scales, range(1))
+        nc.sync.dma_start(x_table[:], x_words[0].rearrange("p c r -> p (c r)").bitcast(I32))
+        scale_rows(raw_plane[0], w1_scales, range(1, 4))
+        scale_rows(raw_plane[1], w2_scales, range(4))
         nc.sync.dma_start(use_t[:], use)
         nc.sync.dma_start(alt1_t[:], alt1)
-        nc.sync.dma_start(raw_words[1][:].bitcast(I32), w2_words[0].bitcast(I32))
-        scale_rows([nc.sync] * 4, raw_plane[1], w2_scales)
-        nc.gpsimd.dma_start(unit_t[:], unit.rearrange("(p t) o -> p (t o)", t=PACK))
         nc.sync.dma_start(alt2_t[:], alt2)
         nc.sync.dma_start(raw_words[2][:].bitcast(I32), w3_words[0].bitcast(I32))
-        scale_rows([nc.sync] * 4, raw_plane[2], w3_scales)
+        scale_rows(raw_plane[2], w3_scales, range(4))
 
         def deal_words(w):
+            w_words[w] = keep.tile([P, 2 * S], U8, name="w_words", bufs=2, align_bytes=64)
             if DEAL[w] == "V":
                 nc.vector.tensor_copy(w_words[w][:].rearrange("p (t m b) -> p t m b", t=PACK, b=2), raw_words[w][:].rearrange("p (m t b) -> p t m b", t=PACK, b=2))
             else:
                 nc.scalar.copy(w_words[w][:].bitcast(U16).rearrange("p (t m) -> p t m", t=PACK), raw_words[w][:].bitcast(U16).rearrange("p (m t) -> p t m", t=PACK))
 
         def deal_plane(w):
+            w_plane[w] = keep.tile([P, S], U8, name="w_plane", bufs=2, align_bytes=64)
             nc.vector.tensor_copy(w_plane[w][:].rearrange("p (t m) -> p t m", t=PACK), raw_plane[w][:].rearrange("p (m t) -> p t m", t=PACK))
 
         def product(acc, w, t, codes, plane):
@@ -121,31 +127,34 @@ def tile_picked_ytoolrt_gate_po_kernel(tc, x_words, x_scales, w1_words, w1_scale
 
         starts = [sum(CHUNKS[:c]) for c in range(len(CHUNKS))]
 
-        def larger(c, t):
+        def fetch(c, t):
             c0, n = starts[c], CHUNKS[c]
             lists = slice(c0 // 16, (c0 + n) // 16)
-            used = keep.tile([P, n], F32, name="used", bufs=RING)
-            other = keep.tile([P, n], F32, name="other", bufs=RING)
-            best = keep.tile([P, n], F32, name="best", bufs=BEST)
-            nc.scalar.activation(used[:], y[t][:].indirect(use_t[:, lists]), COPY)
-            nc.scalar.activation(other[:], y[t][:].indirect(alt1_t[:, lists]), COPY)
-            nc.vector.tensor_tensor(best[:], used[:], other[:], ALU.max)
-            return best
-
-        def gate(hid, c, t, best):
-            c0, n = starts[c], CHUNKS[c]
-            lists = slice(c0 // 16, (c0 + n) // 16)
-            nc.vector.tensor_tensor(hid[:, t, :], z[t][:].indirect(alt2_t[:, lists]), best[:], ALU.mult)
+            if t % PAIR == 0:
+                held = c - 2 if c >= 2 and HOLD and t == 0 else f"{c}_{t}"
+                used[c] = keep.tile([P, PAIR, n], F32, name="used", tag=f"codes{held}", align_bytes=64)
+                other[c] = keep.tile([P, PAIR, n], F32, name="other", tag=f"plane{held}", align_bytes=64)
+            if t == 0:
+                best[c] = keep.tile([P, PACK, n], F32, name="best", tag=f"hid16_{c - 1}" if CHAIN else f"best{c}", align_bytes=64)
+                third[c] = keep.tile([P, PACK, n], F32, name="third", bufs=THIRD)
+            nc.scalar.activation(used[c][:, t % PAIR, :], y[t][:].indirect(use_t[:, lists]), COPY)
+            nc.scalar.activation(other[c][:, t % PAIR, :], y[t][:].indirect(alt1_t[:, lists]), COPY)
+            if (c, t) in Z_ON_SCALAR:
+                nc.scalar.activation(third[c][:, t, :], z[t][:].indirect(alt2_t[:, lists]), COPY)
+            else:
+                nc.vector.tensor_copy(third[c][:, t, :], z[t][:].indirect(alt2_t[:, lists]))
+            if t % PAIR == PAIR - 1:
+                nc.vector.tensor_tensor(best[c][:, t + 1 - PAIR : t + 1, :], used[c][:], other[c][:], ALU.max)
 
         def round_hid(c):
             n = CHUNKS[c]
-            hid16[c] = keep.tile([P, PACK * n], BF16, name=f"hid16_{c}", align_bytes=64)
-            interleave(hid16[c][:], hid[c][:])
+            hid16[c] = keep.tile([P, PACK * n], BF16, name="hid16", tag=f"hid16_{c}", align_bytes=64)
+            nc.vector.tensor_tensor(hid16[c][:].rearrange("p (c i t) -> p c t i", i=4, t=PACK), best[c][:].rearrange("p t (c i) -> p c t i", i=4), third[c][:].rearrange("p t (c i) -> p c t i", i=4), ALU.mult)
 
         def last_product(c):
             n = CHUNKS[c]
             codes = keep.tile([P, n], U32, name="codes", tag=f"codes{c}", align_bytes=64)
-            plane = keep.tile([P, n], U8, name=f"plane_{c}", align_bytes=64)
+            plane = keep.tile([P, n], U8, name="plane", tag=f"plane{c}", align_bytes=64)
             nc.vector.quantize_mx(out=codes[:].bitcast(FP8X4), scales=plane[:], in_=hid16[c][:])
             banks[c] = [psum.tile([P, BANK], F32, name="acc") for b in range(PACK * n // BANK)]
             for t in range(PACK):
@@ -173,24 +182,19 @@ def tile_picked_ytoolrt_gate_po_kernel(tc, x_words, x_scales, w1_words, w1_scale
             nc.vector.quantize_mx(out=out_codes[:, c0 : c0 + n].bitcast(FP8X4), scales=out_plane[:, c0 : c0 + n], in_=res16[c][:])
             nc.sync.dma_start(out_words[:, c0 : c0 + n], out_codes[:, c0 : c0 + n].bitcast(I32))
 
-        hid, hid16, banks, res, res16, best = {}, {}, {}, {}, {}, {}
+        hid16, banks, res, res16, used, other, best, third = {}, {}, {}, {}, {}, {}, {}, {}
         stages = [round_hid, last_product, leave_psum, round_out, hand_on]
         steps = PACK * len(CHUNKS)
-        for step in range(steps + LAG + max(AFTER)):
+        for step in range(steps + max(AFTER)):
             c, t = divmod(step, PACK)
             for stage, after in zip(stages, AFTER):
-                done, rest = divmod(step - LAG - after - (PACK - 1), PACK)
+                done, rest = divmod(step - after - (PACK - 1), PACK)
                 if rest == 0 and 0 <= done < len(CHUNKS):
                     stage(done)
             if step < steps:
                 if step < Y_ON_SCALAR:
                     nc.scalar.copy(y[t][:, :S], y_banks[t][:])
-                if t == 0:
-                    hid[c] = keep.tile([P, PACK, CHUNKS[c]], F32, name=f"hid_{c}")
-                best[step] = larger(c, t)
-            if 0 <= step - LAG < steps:
-                c, t = divmod(step - LAG, PACK)
-                gate(hid[c], c, t, best[step - LAG])
+                fetch(c, t)
         for q in range(4):
             queue = nc.sync if q % 2 else nc.scalar
             queue.dma_start(out_2[0, 4 * q : 4 * q + 4, :].bitcast(I32), out_plane[32 * q : 32 * q + 4, :].bitcast(I32))

@@ -17,17 +17,20 @@ P = 128
 PACK = 4
 T, S, U = 2048, 512, 1024
 FLOPS = 2 * 512 * 512 * (S + S + U)
-CHUNKS = [512, 384, 128]
+PIECES = [[256, 256], [256, 128], [128]]
+LATE = 2
 SPARE = 16
-HOLD = True
+AFTER_TAG = {}
+EARLY3 = 0
+HOLD = {2: "00"}
 THIRD = 2
-CHAIN = True
-ROUND_ON_SCALAR = []
+CHAIN = False
+ROUND_ON_SCALAR = [(1, 0)]
 DEAL = "SSV"
 RING = 3
 BEST = 2
-PAIR = 4
-Z_ON_SCALAR = [(1, 3), (2, 3), (2, 2)]
+PAIR = 2
+Z_ON_SCALAR = [(1, 3)]
 AFTER = [1, 2, 3, 5, 6]
 Y_ON_SCALAR = 1
 BANK = 512
@@ -62,7 +65,11 @@ def tile_picked_ytoolrt_gate_po_kernel(tc, x_words, x_scales, w1_words, w1_scale
         nc.sync.dma_start(offs_t[:], offs)
         nc.sync.dma_start(raw_words[0][:].bitcast(I32), w1_words[0].bitcast(I32))
         nc.gpsimd.dma_start(raw_words[1][:].bitcast(I32), w2_words[0].bitcast(I32))
+        if EARLY3 == 1:
+            nc.gpsimd.dma_start(raw_words[2][:].bitcast(I32), w3_words[0].bitcast(I32))
         nc.gpsimd.dma_start(unit_t[:], unit.rearrange("(p t) o -> p (t o)", t=PACK))
+        if EARLY3 == 2:
+            nc.gpsimd.dma_start(raw_words[2][:].bitcast(I32), w3_words[0].bitcast(I32))
         scale_rows(x_plane, x_scales, range(4))
         scale_rows(raw_plane[0], w1_scales, range(1))
         nc.sync.dma_start(x_table[:], x_words[0].rearrange("p c r -> p (c r)").bitcast(I32))
@@ -71,11 +78,12 @@ def tile_picked_ytoolrt_gate_po_kernel(tc, x_words, x_scales, w1_words, w1_scale
         nc.sync.dma_start(use_t[:], use)
         nc.sync.dma_start(alt1_t[:], alt1)
         nc.sync.dma_start(alt2_t[:], alt2)
-        nc.sync.dma_start(raw_words[2][:].bitcast(I32), w3_words[0].bitcast(I32))
+        if not EARLY3:
+            nc.sync.dma_start(raw_words[2][:].bitcast(I32), w3_words[0].bitcast(I32))
         scale_rows(raw_plane[2], w3_scales, range(4))
 
         def deal_words(w):
-            w_words[w] = keep.tile([P, 2 * S], U8, name="w_words", bufs=2, align_bytes=64)
+            w_words[w] = keep.tile([P, 2 * S], U8, name="w_words", bufs=3 if EARLY3 else 2, align_bytes=64)
             if DEAL[w] == "V":
                 nc.vector.tensor_copy(w_words[w][:].rearrange("p (t m b) -> p t m b", t=PACK, b=2), raw_words[w][:].rearrange("p (m t b) -> p t m b", t=PACK, b=2))
             else:
@@ -98,7 +106,7 @@ def tile_picked_ytoolrt_gate_po_kernel(tc, x_words, x_scales, w1_words, w1_scale
         deal_words(1)
         deal_plane(1)
 
-        spare = SPARE if max(CHUNKS) == S else 0
+        spare = SPARE if max(sum(g) for g in PIECES) == S else 0
         y = [keep.tile([P, S + spare], F32, name=f"y{t}") for t in range(PACK)]
         z = [keep.tile([P, S + spare], F32, name=f"z{t}") for t in range(PACK)]
         for window in y + z:
@@ -125,76 +133,85 @@ def tile_picked_ytoolrt_gate_po_kernel(tc, x_words, x_scales, w1_words, w1_scale
         def interleave(dst, src, on_scalar=False):
             (nc.scalar.copy if on_scalar else nc.vector.tensor_copy)(dst.rearrange("p (c i t) -> p c t i", i=4, t=PACK), src.rearrange("p t (c i) -> p c t i", i=4))
 
-        starts = [sum(CHUNKS[:c]) for c in range(len(CHUNKS))]
+        groups = [sum(g) for g in PIECES]
+        starts = [sum(groups[:g]) for g in range(len(groups))]
+        used, other, third, best, hid16, banks, res, res16 = {}, {}, {}, {}, {}, {}, {}, {}
 
-        def fetch(c, t):
-            c0, n = starts[c], CHUNKS[c]
+        def fetch(g):
+            c0, n = starts[g], groups[g]
             lists = slice(c0 // 16, (c0 + n) // 16)
-            if t % PAIR == 0:
-                held = c - 2 if c >= 2 and HOLD and t == 0 else f"{c}_{t}"
-                used[c] = keep.tile([P, PAIR, n], F32, name="used", tag=f"codes{held}", align_bytes=64)
-                other[c] = keep.tile([P, PAIR, n], F32, name="other", tag=f"plane{held}", align_bytes=64)
-            if t == 0:
-                best[c] = keep.tile([P, PACK, n], F32, name="best", tag=f"hid16_{c - 1}" if CHAIN else f"best{c}", align_bytes=64)
-                third[c] = keep.tile([P, PACK, n], F32, name="third", bufs=THIRD)
-            nc.scalar.activation(used[c][:, t % PAIR, :], y[t][:].indirect(use_t[:, lists]), COPY)
-            nc.scalar.activation(other[c][:, t % PAIR, :], y[t][:].indirect(alt1_t[:, lists]), COPY)
-            if (c, t) in Z_ON_SCALAR:
-                nc.scalar.activation(third[c][:, t, :], z[t][:].indirect(alt2_t[:, lists]), COPY)
-            else:
-                nc.vector.tensor_copy(third[c][:, t, :], z[t][:].indirect(alt2_t[:, lists]))
-            if t % PAIR == PAIR - 1:
-                nc.vector.tensor_tensor(best[c][:, t + 1 - PAIR : t + 1, :], used[c][:], other[c][:], ALU.max)
-
-        def round_hid(c):
-            n = CHUNKS[c]
-            hid16[c] = keep.tile([P, PACK * n], BF16, name="hid16", tag=f"hid16_{c}", align_bytes=64)
-            nc.vector.tensor_tensor(hid16[c][:].rearrange("p (c i t) -> p c t i", i=4, t=PACK), best[c][:].rearrange("p t (c i) -> p c t i", i=4), third[c][:].rearrange("p t (c i) -> p c t i", i=4), ALU.mult)
-
-        def last_product(c):
-            n = CHUNKS[c]
-            codes = keep.tile([P, n], U32, name="codes", tag=f"codes{c}", align_bytes=64)
-            plane = keep.tile([P, n], U8, name="plane", tag=f"plane{c}", align_bytes=64)
-            nc.vector.quantize_mx(out=codes[:].bitcast(FP8X4), scales=plane[:], in_=hid16[c][:])
-            banks[c] = [psum.tile([P, BANK], F32, name="acc") for b in range(PACK * n // BANK)]
+            held = HOLD.get(g, f"free{g}")
+            used[g] = keep.tile([P, PACK, n], F32, name="used", tag=f"codes{held}", align_bytes=64)
+            other[g] = keep.tile([P, PACK, n], F32, name="other", tag=f"plane{held}", align_bytes=64)
+            third[g] = keep.tile([P, PACK, n], F32, name="third", bufs=THIRD)
             for t in range(PACK):
-                j = 0
-                while j < n:
-                    b, at = divmod(t * n + j, BANK)
-                    width = max(w for w in (128, 256, 512) if w <= min(n - j, BANK - at))
-                    product(banks[c][b][:, at : at + width], 2, t, codes[:, j : j + width], plane[:, j : j + width])
-                    j += width
-
-        def leave_psum(c):
-            c0, n = starts[c], CHUNKS[c]
-            res[c] = keep.tile([P, PACK, n], F32, name=f"res_{c}")
-            flat = res[c][:].rearrange("p t n -> p (t n)")
-            for b, acc in enumerate(banks[c]):
-                nc.scalar.copy(flat[:, b * BANK : (b + 1) * BANK], acc[:])
-            nc.sync.dma_start(out_rows[:, :, c0 : c0 + n], res[c][:])
-
-        def round_out(c):
-            res16[c] = keep.tile([P, PACK * CHUNKS[c]], BF16, name=f"res16_{c}", align_bytes=64)
-            interleave(res16[c][:], res[c][:], c in ROUND_ON_SCALAR)
-
-        def hand_on(c):
-            c0, n = starts[c], CHUNKS[c]
-            nc.vector.quantize_mx(out=out_codes[:, c0 : c0 + n].bitcast(FP8X4), scales=out_plane[:, c0 : c0 + n], in_=res16[c][:])
-            nc.sync.dma_start(out_words[:, c0 : c0 + n], out_codes[:, c0 : c0 + n].bitcast(I32))
-
-        hid16, banks, res, res16, used, other, best, third = {}, {}, {}, {}, {}, {}, {}, {}
-        stages = [round_hid, last_product, leave_psum, round_out, hand_on]
-        steps = PACK * len(CHUNKS)
-        for step in range(steps + max(AFTER)):
-            c, t = divmod(step, PACK)
-            for stage, after in zip(stages, AFTER):
-                done, rest = divmod(step - after - (PACK - 1), PACK)
-                if rest == 0 and 0 <= done < len(CHUNKS):
-                    stage(done)
-            if step < steps:
-                if step < Y_ON_SCALAR:
+                if g == 0 and t < Y_ON_SCALAR:
                     nc.scalar.copy(y[t][:, :S], y_banks[t][:])
-                fetch(c, t)
+                nc.scalar.activation(used[g][:, t, :], y[t][:].indirect(use_t[:, lists]), COPY)
+                nc.scalar.activation(other[g][:, t, :], y[t][:].indirect(alt1_t[:, lists]), COPY)
+                if (g, t) in Z_ON_SCALAR:
+                    nc.scalar.activation(third[g][:, t, :], z[t][:].indirect(alt2_t[:, lists]), COPY)
+                else:
+                    nc.vector.tensor_copy(third[g][:, t, :], z[t][:].indirect(alt2_t[:, lists]))
+
+        def inside(g, j):
+            a = sum(PIECES[g][:j])
+            return slice(a, a + PIECES[g][j])
+
+        def larger(g, j):
+            n = PIECES[g][j]
+            best[g, j] = keep.tile([P, PACK, n], F32, name="best", tag=f"hid16_{g - 1}_{len(PIECES[g - 1]) - 1}" if CHAIN and j == 0 and g else f"best{g}{j}", align_bytes=64)
+            nc.vector.tensor_tensor(best[g, j][:], used[g][:, :, inside(g, j)], other[g][:, :, inside(g, j)], ALU.max)
+
+        def round_hid(g, j):
+            n = PIECES[g][j]
+            hid16[g, j] = keep.tile([P, PACK * n], BF16, name="hid16", tag=f"hid16_{g}_{j}", align_bytes=64)
+            nc.vector.tensor_tensor(hid16[g, j][:].rearrange("p (c i t) -> p c t i", i=4, t=PACK), best[g, j][:].rearrange("p t (c i) -> p c t i", i=4), third[g][:, :, inside(g, j)].rearrange("p t (c i) -> p c t i", i=4), ALU.mult)
+
+        def last_product(g, j):
+            n = PIECES[g][j]
+            codes = keep.tile([P, n], U32, name="codes", tag=f"codes{g}{j}", align_bytes=64)
+            plane = keep.tile([P, n], U8, name="plane", tag=f"plane{g}{j}", align_bytes=64)
+            nc.vector.quantize_mx(out=codes[:].bitcast(FP8X4), scales=plane[:], in_=hid16[g, j][:])
+            banks[g, j] = [psum.tile([P, BANK], F32, name="acc") for b in range(PACK * n // BANK)]
+            for t in range(PACK):
+                b, at = divmod(t * n, BANK)
+                product(banks[g, j][b][:, at : at + n], 2, t, codes[:], plane[:])
+
+        def leave_psum(g, j):
+            c0, n = starts[g] + inside(g, j).start, PIECES[g][j]
+            res[g, j] = keep.tile([P, PACK, n], F32, name=f"res_{g}{j}")
+            flat = res[g, j][:].rearrange("p t n -> p (t n)")
+            for b, acc in enumerate(banks[g, j]):
+                nc.scalar.copy(flat[:, b * BANK : (b + 1) * BANK], acc[:])
+            nc.sync.dma_start(out_rows[:, :, c0 : c0 + n], res[g, j][:])
+
+        def round_out(g, j):
+            res16[g, j] = keep.tile([P, PACK * PIECES[g][j]], BF16, name="res16", tag=AFTER_TAG.get((g, j), f"res16_{g}{j}"), align_bytes=64)
+            interleave(res16[g, j][:], res[g, j][:], (g, j) in ROUND_ON_SCALAR)
+
+        def hand_on(g, j):
+            c0, n = starts[g] + inside(g, j).start, PIECES[g][j]
+            nc.vector.quantize_mx(out=out_codes[:, c0 : c0 + n].bitcast(FP8X4), scales=out_plane[:, c0 : c0 + n], in_=res16[g, j][:])
+            if j == len(PIECES[g]) - 1:
+                cols = slice(starts[g], starts[g] + groups[g])
+                nc.sync.dma_start(out_words[:, cols], out_codes[:, cols].bitcast(I32))
+
+        def each(stages, g):
+            if 0 <= g < len(PIECES):
+                for stage in stages:
+                    for j in range(len(PIECES[g])):
+                        stage(g, j)
+
+        for g in range(len(PIECES) + 2):
+            each([larger, round_hid, last_product, leave_psum], g - 1)
+            if LATE < 2:
+                each([round_out, hand_on], g - 1 - LATE)
+            if g < len(PIECES):
+                fetch(g)
+        if LATE == 2:
+            for g in range(len(PIECES)):
+                each([round_out, hand_on], g)
         for q in range(4):
             queue = nc.sync if q % 2 else nc.scalar
             queue.dma_start(out_2[0, 4 * q : 4 * q + 4, :].bitcast(I32), out_plane[32 * q : 32 * q + 4, :].bitcast(I32))

@@ -15,36 +15,27 @@ COPY = mybir.ActivationFunctionType.Copy
 
 P = 128
 PACK = 4
-T, S, U = 2048, 512, 1024
-FLOPS = 2 * 512 * 512 * (S + S + U)
-PIECES = [[256, 256], [256, 128], [128]]
-LATE = 2
-SPARE = 16
-AFTER_TAG = {}
-EARLY3 = 0
-HOLD = {2: "00"}
-THIRD = 2
-CHAIN = False
-ROUND_ON_SCALAR = [(1, 0)]
-DEAL = "SSV"
-RING = 3
-BEST = 2
-PAIR = 2
-Z_ON_SCALAR = [(1, 3)]
-AFTER = [1, 2, 3, 5, 6]
-Y_ON_SCALAR = 1
+QUADRANTS = 4
+LINE = 4
 BANK = 512
+T, S, U = 2048, 512, 1024
+HALF = S // 2
+FLOPS = 2 * 512 * 512 * (S + S + U)
+W1, W2, W3 = 0, 1, 2
+
+PIECES = [[256, 256], [256, 128], [128]]
+SPARE = 16
+SHARE = 256
+ROUNDED_ON_SCALAR = (1, 0)
 
 
-def tile_picked_ytoolrt_gate_po_kernel(tc, x_words, x_scales, w1_words, w1_scales, w2_words, w2_scales, unit, w3_words, w3_scales, offs, use, alt1, alt2, out_0, out_1, out_2):
+def tile_picked_ytoolrt_gate_po_kernel(
+    tc, x_words, x_scales, w1_words, w1_scales, w2_words, w2_scales, unit, w3_words, w3_scales, offs, use, alt1, alt2, out_0, out_1, out_2
+):
     nc = tc.nc
     with ExitStack() as ctx:
         keep = ctx.enter_context(tc.tile_pool(name="keep", bufs=1))
         psum = ctx.enter_context(tc.psum_pool(name="psum", bufs=8))
-
-        def scale_rows(plane, scales, quadrants):
-            for q in quadrants:
-                nc.sync.dma_start(plane[32 * q : 32 * q + 4, :].bitcast(I32), scales[0, 4 * q : 4 * q + 4, :].bitcast(I32))
 
         offs_t = keep.tile([P, S // 16], U16, name="offs_t")
         use_t = keep.tile([P, U // 16], U16, name="use_t")
@@ -53,120 +44,149 @@ def tile_picked_ytoolrt_gate_po_kernel(tc, x_words, x_scales, w1_words, w1_scale
         x_table = keep.tile([P, T], I32, name="x_table", align_bytes=64)
         x_plane = keep.tile([P, T], U8, name="x_plane", align_bytes=64)
         unit_t = keep.tile([P, PACK], F32, name="unit_t")
-        raw_words = [keep.tile([P, 2 * S], U8, name=f"raw_words{w}", align_bytes=64) for w in range(3)]
-        raw_plane = [keep.tile([P, S], U8, name=f"raw_plane{w}", align_bytes=64) for w in range(3)]
-        w_words, w_plane = {}, {}
+        raw_words = [keep.tile([P, 2 * S], U8, name=f"raw_words{w}", align_bytes=64) for w in (W1, W2, W3)]
+        raw_plane = [keep.tile([P, S], U8, name=f"raw_plane{w}", align_bytes=64) for w in (W1, W2, W3)]
 
         nc.vector.memset(x_plane[:].bitcast(I32), 0)
-        nc.vector.memset(raw_plane[0][:].bitcast(I32), 0)
-        nc.vector.memset(raw_plane[1][:].bitcast(I32), 0)
-        nc.vector.memset(raw_plane[2][:].bitcast(I32), 0)
+        for plane in raw_plane:
+            nc.vector.memset(plane[:].bitcast(I32), 0)
+
+        def load_bytes(queue, tile, source):
+            queue.dma_start(tile.bitcast(I32), source.bitcast(I32))
+
+        def load_scales(plane, scales, quadrants):
+            for q in quadrants:
+                load_bytes(nc.sync, plane[32 * q : 32 * q + 4, :], scales[0, 4 * q : 4 * q + 4, :])
 
         nc.sync.dma_start(offs_t[:], offs)
-        nc.sync.dma_start(raw_words[0][:].bitcast(I32), w1_words[0].bitcast(I32))
-        nc.gpsimd.dma_start(raw_words[1][:].bitcast(I32), w2_words[0].bitcast(I32))
-        if EARLY3 == 1:
-            nc.gpsimd.dma_start(raw_words[2][:].bitcast(I32), w3_words[0].bitcast(I32))
+        load_bytes(nc.sync, raw_words[W1][:], w1_words[0])
+        load_bytes(nc.gpsimd, raw_words[W2][:], w2_words[0])
         nc.gpsimd.dma_start(unit_t[:], unit.rearrange("(p t) o -> p (t o)", t=PACK))
-        if EARLY3 == 2:
-            nc.gpsimd.dma_start(raw_words[2][:].bitcast(I32), w3_words[0].bitcast(I32))
-        scale_rows(x_plane, x_scales, range(4))
-        scale_rows(raw_plane[0], w1_scales, range(1))
+        load_scales(x_plane, x_scales, range(QUADRANTS))
+        load_scales(raw_plane[W1], w1_scales, range(1))
         nc.sync.dma_start(x_table[:], x_words[0].rearrange("p c r -> p (c r)").bitcast(I32))
-        scale_rows(raw_plane[0], w1_scales, range(1, 4))
-        scale_rows(raw_plane[1], w2_scales, range(4))
+        load_scales(raw_plane[W1], w1_scales, range(1, QUADRANTS))
+        load_scales(raw_plane[W2], w2_scales, range(QUADRANTS))
         nc.sync.dma_start(use_t[:], use)
         nc.sync.dma_start(alt1_t[:], alt1)
         nc.sync.dma_start(alt2_t[:], alt2)
-        if not EARLY3:
-            nc.sync.dma_start(raw_words[2][:].bitcast(I32), w3_words[0].bitcast(I32))
-        scale_rows(raw_plane[2], w3_scales, range(4))
+        load_bytes(nc.sync, raw_words[W3][:], w3_words[0])
+        load_scales(raw_plane[W3], w3_scales, range(QUADRANTS))
+
+        w_words, w_plane = {}, {}
 
         def deal_words(w):
-            w_words[w] = keep.tile([P, 2 * S], U8, name="w_words", bufs=3 if EARLY3 else 2, align_bytes=64)
-            if DEAL[w] == "V":
-                nc.vector.tensor_copy(w_words[w][:].rearrange("p (t m b) -> p t m b", t=PACK, b=2), raw_words[w][:].rearrange("p (m t b) -> p t m b", t=PACK, b=2))
+            w_words[w] = keep.tile([P, 2 * S], U8, name="w_words", bufs=3, align_bytes=64)
+            if w == W3:
+                nc.gpsimd.tensor_copy(
+                    w_words[w][:].rearrange("p (t m b) -> p t m b", t=PACK, b=2),
+                    raw_words[w][:].rearrange("p (m t b) -> p t m b", t=PACK, b=2),
+                )
             else:
-                nc.scalar.copy(w_words[w][:].bitcast(U16).rearrange("p (t m) -> p t m", t=PACK), raw_words[w][:].bitcast(U16).rearrange("p (m t) -> p t m", t=PACK))
+                nc.scalar.copy(
+                    w_words[w][:].bitcast(U16).rearrange("p (t m) -> p t m", t=PACK),
+                    raw_words[w][:].bitcast(U16).rearrange("p (m t) -> p t m", t=PACK),
+                )
 
         def deal_plane(w):
-            w_plane[w] = keep.tile([P, S], U8, name="w_plane", bufs=2, align_bytes=64)
-            nc.vector.tensor_copy(w_plane[w][:].rearrange("p (t m) -> p t m", t=PACK), raw_plane[w][:].rearrange("p (m t) -> p t m", t=PACK))
+            w_plane[w] = keep.tile([P, S], U8, name="w_plane", bufs=3, align_bytes=64)
+            engine = nc.gpsimd if w == W3 else nc.vector
+            engine.tensor_copy(
+                w_plane[w][:].rearrange("p (t m) -> p t m", t=PACK),
+                raw_plane[w][:].rearrange("p (m t) -> p t m", t=PACK),
+            )
 
         def product(acc, w, t, codes, plane):
-            nc.tensor.matmul_mx(out=acc, lhsT=w_words[w][:, 2 * P * t : 2 * P * (t + 1)].bitcast(FP4X4), lhsT_scale=w_plane[w][:, P * t : P * (t + 1)],
-                                rhs=codes.bitcast(FP8X4), rhs_scale=plane, start=True, stop=True)
+            nc.tensor.matmul_mx(
+                out=acc,
+                lhsT=w_words[w][:, 2 * P * t : 2 * P * (t + 1)].bitcast(FP4X4),
+                lhsT_scale=w_plane[w][:, P * t : P * (t + 1)],
+                rhs=codes.bitcast(FP8X4),
+                rhs_scale=plane,
+                start=True,
+                stop=True,
+            )
 
+        halves = [slice(0, HALF), slice(HALF, S)]
         xq_words = keep.tile([P, S], U32, name="xq_words", align_bytes=64)
         xq_plane = keep.tile([P, S], U8, name="xq_plane", align_bytes=64)
-        deal_words(0)
+        deal_words(W1)
         nc.vector.tensor_copy(xq_plane[:], x_plane[:].indirect(offs_t[:]))
-        deal_plane(0)
-        nc.vector.tensor_copy(xq_words[:], x_table[:].bitcast(U32).indirect(offs_t[:]))
-        deal_words(1)
-        deal_plane(1)
+        deal_plane(W1)
+        for half in halves:
+            nc.vector.tensor_copy(xq_words[:, half], x_table[:].bitcast(U32).indirect(offs_t[:, half.start // 16 : half.stop // 16]))
+        deal_words(W2)
+        deal_plane(W2)
 
-        spare = SPARE if max(sum(g) for g in PIECES) == S else 0
-        y = [keep.tile([P, S + spare], F32, name=f"y{t}") for t in range(PACK)]
-        z = [keep.tile([P, S + spare], F32, name=f"z{t}") for t in range(PACK)]
+        y = [keep.tile([P, S + SPARE], F32, name=f"y{t}") for t in range(PACK)]
+        z = [keep.tile([P, S + SPARE], F32, name=f"z{t}") for t in range(PACK)]
         for window in y + z:
-            if spare:
-                nc.gpsimd.memset(window[:, S:], 0.0)
-        y_banks = []
+            nc.gpsimd.memset(window[:, S:], 0.0)
+        for half, leave in zip(halves, (nc.vector.tensor_copy, nc.scalar.copy)):
+            acc = psum.tile([P, BANK], F32, name="acc")
+            product(acc[:, :HALF], W1, 0, xq_words[:, half], xq_plane[:, half])
+            leave(y[0][:, half], acc[:, :HALF])
+        for t in range(1, PACK):
+            acc = psum.tile([P, BANK], F32, name="acc")
+            product(acc[:], W1, t, xq_words[:], xq_plane[:])
+            nc.vector.tensor_copy(y[t][:, :S], acc[:])
         for t in range(PACK):
             acc = psum.tile([P, BANK], F32, name="acc")
-            product(acc[:], 0, t, xq_words[:], xq_plane[:])
-            y_banks.append(acc)
-            if t >= Y_ON_SCALAR:
-                nc.vector.tensor_copy(y[t][:, :S], acc[:])
-            acc = psum.tile([P, BANK], F32, name="acc")
-            product(acc[:], 1, t, xq_words[:], xq_plane[:])
+            product(acc[:], W2, t, xq_words[:], xq_plane[:])
             nc.vector.tensor_scalar(z[t][:, :S], acc[:], unit_t[:, t : t + 1], None, ALU.mult)
-        deal_words(2)
-        deal_plane(2)
+        deal_words(W3)
+        deal_plane(W3)
 
         out_codes = keep.tile([P, U], U32, name="out_codes", align_bytes=64)
         out_plane = keep.tile([P, U], U8, name="out_plane", align_bytes=64)
         out_rows = out_0.rearrange("(p t) r -> p t r", t=PACK)
         out_words = out_1[0].rearrange("p c r -> p (c r)").bitcast(I32)
 
-        def interleave(dst, src, on_scalar=False):
-            (nc.scalar.copy if on_scalar else nc.vector.tensor_copy)(dst.rearrange("p (c i t) -> p c t i", i=4, t=PACK), src.rearrange("p t (c i) -> p c t i", i=4))
+        def as_row_sets(tile):
+            return tile.rearrange("p t (c i) -> p c t i", i=LINE)
 
-        groups = [sum(g) for g in PIECES]
-        starts = [sum(groups[:g]) for g in range(len(groups))]
+        def as_interleaved(tile):
+            return tile.rearrange("p (c i t) -> p c t i", i=LINE, t=PACK)
+
+        widths = [sum(pieces) for pieces in PIECES]
+        starts = [sum(widths[:g]) for g in range(len(PIECES))]
+        last_group = len(PIECES) - 1
         used, other, third, best, hid16, banks, res, res16 = {}, {}, {}, {}, {}, {}, {}, {}
 
-        def fetch(g):
-            c0, n = starts[g], groups[g]
-            lists = slice(c0 // 16, (c0 + n) // 16)
-            held = HOLD.get(g, f"free{g}")
-            used[g] = keep.tile([P, PACK, n], F32, name="used", tag=f"codes{held}", align_bytes=64)
-            other[g] = keep.tile([P, PACK, n], F32, name="other", tag=f"plane{held}", align_bytes=64)
-            third[g] = keep.tile([P, PACK, n], F32, name="third", bufs=THIRD)
-            for t in range(PACK):
-                if g == 0 and t < Y_ON_SCALAR:
-                    nc.scalar.copy(y[t][:, :S], y_banks[t][:])
-                nc.scalar.activation(used[g][:, t, :], y[t][:].indirect(use_t[:, lists]), COPY)
-                nc.scalar.activation(other[g][:, t, :], y[t][:].indirect(alt1_t[:, lists]), COPY)
-                if (g, t) in Z_ON_SCALAR:
-                    nc.scalar.activation(third[g][:, t, :], z[t][:].indirect(alt2_t[:, lists]), COPY)
-                else:
-                    nc.vector.tensor_copy(third[g][:, t, :], z[t][:].indirect(alt2_t[:, lists]))
+        def entries(list_tile, first, count):
+            return list_tile[:, first // 16 : (first + count) // 16]
 
         def inside(g, j):
-            a = sum(PIECES[g][:j])
-            return slice(a, a + PIECES[g][j])
+            first = sum(PIECES[g][:j])
+            return slice(first, first + PIECES[g][j])
+
+        def fetch(g):
+            first, n = starts[g], widths[g]
+            buffer = "00" if g == last_group else f"group{g}"
+            used[g] = keep.tile([P, PACK, n], F32, name="used", tag=f"codes{buffer}", align_bytes=64)
+            other[g] = keep.tile([P, PACK, n], F32, name="other", tag=f"plane{buffer}", align_bytes=64)
+            third[g] = keep.tile([P, PACK, n], F32, name="third")
+            for t in range(PACK):
+                nc.scalar.activation(used[g][:, t, :], y[t][:].indirect(entries(use_t, first, n)), COPY)
+                own = n
+                if g == 0 and t == PACK - 1:
+                    own = n - SHARE
+                    nc.vector.tensor_copy(other[g][:, t, own:], y[t][:].indirect(entries(alt1_t, first + own, SHARE)))
+                nc.scalar.activation(other[g][:, t, :own], y[t][:].indirect(entries(alt1_t, first, own)), COPY)
+                if g > 0 and t == PACK - 1:
+                    nc.scalar.activation(third[g][:, t, :], z[t][:].indirect(entries(alt2_t, first, n)), COPY)
+                else:
+                    nc.vector.tensor_copy(third[g][:, t, :], z[t][:].indirect(entries(alt2_t, first, n)))
 
         def larger(g, j):
-            n = PIECES[g][j]
-            best[g, j] = keep.tile([P, PACK, n], F32, name="best", tag=f"hid16_{g - 1}_{len(PIECES[g - 1]) - 1}" if CHAIN and j == 0 and g else f"best{g}{j}", align_bytes=64)
+            best[g, j] = keep.tile([P, PACK, PIECES[g][j]], F32, name=f"best{g}{j}", align_bytes=64)
             nc.vector.tensor_tensor(best[g, j][:], used[g][:, :, inside(g, j)], other[g][:, :, inside(g, j)], ALU.max)
 
         def round_hid(g, j):
-            n = PIECES[g][j]
-            hid16[g, j] = keep.tile([P, PACK * n], BF16, name="hid16", tag=f"hid16_{g}_{j}", align_bytes=64)
-            nc.vector.tensor_tensor(hid16[g, j][:].rearrange("p (c i t) -> p c t i", i=4, t=PACK), best[g, j][:].rearrange("p t (c i) -> p c t i", i=4), third[g][:, :, inside(g, j)].rearrange("p t (c i) -> p c t i", i=4), ALU.mult)
+            hid16[g, j] = keep.tile([P, PACK * PIECES[g][j]], BF16, name=f"hid16_{g}{j}", align_bytes=64)
+            nc.vector.tensor_tensor(
+                as_interleaved(hid16[g, j][:]), as_row_sets(best[g, j][:]), as_row_sets(third[g][:, :, inside(g, j)]), ALU.mult
+            )
 
         def last_product(g, j):
             n = PIECES[g][j]
@@ -176,42 +196,40 @@ def tile_picked_ytoolrt_gate_po_kernel(tc, x_words, x_scales, w1_words, w1_scale
             banks[g, j] = [psum.tile([P, BANK], F32, name="acc") for b in range(PACK * n // BANK)]
             for t in range(PACK):
                 b, at = divmod(t * n, BANK)
-                product(banks[g, j][b][:, at : at + n], 2, t, codes[:], plane[:])
+                product(banks[g, j][b][:, at : at + n], W3, t, codes[:], plane[:])
 
         def leave_psum(g, j):
-            c0, n = starts[g] + inside(g, j).start, PIECES[g][j]
+            first, n = starts[g] + inside(g, j).start, PIECES[g][j]
             res[g, j] = keep.tile([P, PACK, n], F32, name=f"res_{g}{j}")
             flat = res[g, j][:].rearrange("p t n -> p (t n)")
             for b, acc in enumerate(banks[g, j]):
                 nc.scalar.copy(flat[:, b * BANK : (b + 1) * BANK], acc[:])
-            nc.sync.dma_start(out_rows[:, :, c0 : c0 + n], res[g, j][:])
+            nc.sync.dma_start(out_rows[:, :, first : first + n], res[g, j][:])
 
         def round_out(g, j):
-            res16[g, j] = keep.tile([P, PACK * PIECES[g][j]], BF16, name="res16", tag=AFTER_TAG.get((g, j), f"res16_{g}{j}"), align_bytes=64)
-            interleave(res16[g, j][:], res[g, j][:], (g, j) in ROUND_ON_SCALAR)
+            res16[g, j] = keep.tile([P, PACK * PIECES[g][j]], BF16, name=f"res16_{g}{j}", align_bytes=64)
+            copy = nc.scalar.copy if (g, j) == ROUNDED_ON_SCALAR else nc.vector.tensor_copy
+            copy(as_interleaved(res16[g, j][:]), as_row_sets(res[g, j][:]))
 
         def hand_on(g, j):
-            c0, n = starts[g] + inside(g, j).start, PIECES[g][j]
-            nc.vector.quantize_mx(out=out_codes[:, c0 : c0 + n].bitcast(FP8X4), scales=out_plane[:, c0 : c0 + n], in_=res16[g, j][:])
+            first, n = starts[g] + inside(g, j).start, PIECES[g][j]
+            nc.vector.quantize_mx(
+                out=out_codes[:, first : first + n].bitcast(FP8X4), scales=out_plane[:, first : first + n], in_=res16[g, j][:]
+            )
             if j == len(PIECES[g]) - 1:
-                cols = slice(starts[g], starts[g] + groups[g])
-                nc.sync.dma_start(out_words[:, cols], out_codes[:, cols].bitcast(I32))
+                group = slice(starts[g], starts[g] + widths[g])
+                nc.sync.dma_start(out_words[:, group], out_codes[:, group].bitcast(I32))
 
-        def each(stages, g):
-            if 0 <= g < len(PIECES):
-                for stage in stages:
-                    for j in range(len(PIECES[g])):
-                        stage(g, j)
+        def stage_by_stage(stages, g):
+            for stage in stages:
+                for j in range(len(PIECES[g])):
+                    stage(g, j)
 
-        for g in range(len(PIECES) + 2):
-            each([larger, round_hid, last_product, leave_psum], g - 1)
-            if LATE < 2:
-                each([round_out, hand_on], g - 1 - LATE)
-            if g < len(PIECES):
-                fetch(g)
-        if LATE == 2:
-            for g in range(len(PIECES)):
-                each([round_out, hand_on], g)
-        for q in range(4):
+        for g in range(len(PIECES)):
+            fetch(g)
+            stage_by_stage([larger, round_hid, last_product, leave_psum], g)
+        for g in range(len(PIECES)):
+            stage_by_stage([round_out, hand_on], g)
+        for q in range(QUADRANTS):
             queue = nc.sync if q % 2 else nc.scalar
             queue.dma_start(out_2[0, 4 * q : 4 * q + 4, :].bitcast(I32), out_plane[32 * q : 32 * q + 4, :].bitcast(I32))

from contextlib import ExitStack

import concourse.mybir as mybir

F32 = mybir.dt.float32
BF16 = mybir.dt.bfloat16
I32 = mybir.dt.int32
U32 = mybir.dt.uint32
U16 = mybir.dt.uint16
U8 = mybir.dt.uint8
FP8X4 = mybir.dt.float8_e4m3fn_x4
FP4X4 = mybir.dt.float4_e2m1fn_x4
ALU = mybir.AluOpType
COPY = mybir.ActivationFunctionType.Copy

P = 128
PACK = 4
QUADRANTS = 4
LINE = 4
BANK = 512
T, S, U = 2048, 512, 1024
HALF = S // 2
FLOPS = 2 * 512 * 512 * (S + S + U)
W1, W2, W3 = 0, 1, 2

PIECES = [[256, 256], [256, 128], [128]]
SPARE = 16
SHARE = 256
ROUNDED_ON_SCALAR = (1, 0)


def tile_picked_ytoolrt_gate_po_kernel(
    tc, x_words, x_scales, w1_words, w1_scales, w2_words, w2_scales, unit, w3_words, w3_scales, offs, use, alt1, alt2, out_0, out_1, out_2
):
    nc = tc.nc
    with ExitStack() as ctx:
        keep = ctx.enter_context(tc.tile_pool(name="keep", bufs=1))
        psum = ctx.enter_context(tc.psum_pool(name="psum", bufs=8))

        offs_t = keep.tile([P, S // 16], U16, name="offs_t")
        use_t = keep.tile([P, U // 16], U16, name="use_t")
        alt1_t = keep.tile([P, U // 16], U16, name="alt1_t")
        alt2_t = keep.tile([P, U // 16], U16, name="alt2_t")
        x_table = keep.tile([P, T], I32, name="x_table", align_bytes=64)
        x_plane = keep.tile([P, T], U8, name="x_plane", align_bytes=64)
        unit_t = keep.tile([P, PACK], F32, name="unit_t")
        raw_words = [keep.tile([P, 2 * S], U8, name=f"raw_words{w}", align_bytes=64) for w in (W1, W2, W3)]
        raw_plane = [keep.tile([P, S], U8, name=f"raw_plane{w}", align_bytes=64) for w in (W1, W2, W3)]

        nc.vector.memset(x_plane[:].bitcast(I32), 0)
        for plane in raw_plane:
            nc.vector.memset(plane[:].bitcast(I32), 0)

        def load_bytes(queue, tile, source):
            queue.dma_start(tile.bitcast(I32), source.bitcast(I32))

        def load_scales(plane, scales, quadrants):
            for q in quadrants:
                load_bytes(nc.sync, plane[32 * q : 32 * q + 4, :], scales[0, 4 * q : 4 * q + 4, :])

        nc.sync.dma_start(offs_t[:], offs)
        load_bytes(nc.sync, raw_words[W1][:], w1_words[0])
        load_bytes(nc.gpsimd, raw_words[W2][:], w2_words[0])
        nc.gpsimd.dma_start(unit_t[:], unit.rearrange("(p t) o -> p (t o)", t=PACK))
        load_scales(x_plane, x_scales, range(QUADRANTS))
        load_scales(raw_plane[W1], w1_scales, range(1))
        nc.sync.dma_start(x_table[:], x_words[0].rearrange("p c r -> p (c r)").bitcast(I32))
        load_scales(raw_plane[W1], w1_scales, range(1, QUADRANTS))
        load_scales(raw_plane[W2], w2_scales, range(QUADRANTS))
        nc.sync.dma_start(use_t[:], use)
        nc.sync.dma_start(alt1_t[:], alt1)
        nc.sync.dma_start(alt2_t[:], alt2)
        load_bytes(nc.sync, raw_words[W3][:], w3_words[0])
        load_scales(raw_plane[W3], w3_scales, range(QUADRANTS))

        w_words, w_plane = {}, {}

        def deal_words(w):
            w_words[w] = keep.tile([P, 2 * S], U8, name="w_words", bufs=3, align_bytes=64)
            if w == W3:
                nc.gpsimd.tensor_copy(
                    w_words[w][:].rearrange("p (t m b) -> p t m b", t=PACK, b=2),
                    raw_words[w][:].rearrange("p (m t b) -> p t m b", t=PACK, b=2),
                )
            else:
                nc.scalar.copy(
                    w_words[w][:].bitcast(U16).rearrange("p (t m) -> p t m", t=PACK),
                    raw_words[w][:].bitcast(U16).rearrange("p (m t) -> p t m", t=PACK),
                )

        def deal_plane(w):
            w_plane[w] = keep.tile([P, S], U8, name="w_plane", bufs=3, align_bytes=64)
            engine = nc.gpsimd if w == W3 else nc.vector
            engine.tensor_copy(
                w_plane[w][:].rearrange("p (t m) -> p t m", t=PACK),
                raw_plane[w][:].rearrange("p (m t) -> p t m", t=PACK),
            )

        def product(acc, w, t, codes, plane):
            nc.tensor.matmul_mx(
                out=acc,
                lhsT=w_words[w][:, 2 * P * t : 2 * P * (t + 1)].bitcast(FP4X4),
                lhsT_scale=w_plane[w][:, P * t : P * (t + 1)],
                rhs=codes.bitcast(FP8X4),
                rhs_scale=plane,
                start=True,
                stop=True,
            )

        halves = [slice(0, HALF), slice(HALF, S)]
        xq_words = keep.tile([P, S], U32, name="xq_words", align_bytes=64)
        xq_plane = keep.tile([P, S], U8, name="xq_plane", align_bytes=64)
        deal_words(W1)
        nc.vector.tensor_copy(xq_plane[:], x_plane[:].indirect(offs_t[:]))
        deal_plane(W1)
        for half in halves:
            nc.vector.tensor_copy(xq_words[:, half], x_table[:].bitcast(U32).indirect(offs_t[:, half.start // 16 : half.stop // 16]))
        deal_words(W2)
        deal_plane(W2)

        y = [keep.tile([P, S + SPARE], F32, name=f"y{t}") for t in range(PACK)]
        z = [keep.tile([P, S + SPARE], F32, name=f"z{t}") for t in range(PACK)]
        for window in y + z:
            nc.gpsimd.memset(window[:, S:], 0.0)
        for half, leave in zip(halves, (nc.vector.tensor_copy, nc.scalar.copy)):
            acc = psum.tile([P, BANK], F32, name="acc")
            product(acc[:, :HALF], W1, 0, xq_words[:, half], xq_plane[:, half])
            leave(y[0][:, half], acc[:, :HALF])
        for t in range(1, PACK):
            acc = psum.tile([P, BANK], F32, name="acc")
            product(acc[:], W1, t, xq_words[:], xq_plane[:])
            nc.vector.tensor_copy(y[t][:, :S], acc[:])
        for t in range(PACK):
            acc = psum.tile([P, BANK], F32, name="acc")
            product(acc[:], W2, t, xq_words[:], xq_plane[:])
            nc.vector.tensor_scalar(z[t][:, :S], acc[:], unit_t[:, t : t + 1], None, ALU.mult)
        deal_words(W3)
        deal_plane(W3)

        out_codes = keep.tile([P, U], U32, name="out_codes", align_bytes=64)
        out_plane = keep.tile([P, U], U8, name="out_plane", align_bytes=64)
        out_rows = out_0.rearrange("(p t) r -> p t r", t=PACK)
        out_words = out_1[0].rearrange("p c r -> p (c r)").bitcast(I32)

        def as_row_sets(tile):
            return tile.rearrange("p t (c i) -> p c t i", i=LINE)

        def as_interleaved(tile):
            return tile.rearrange("p (c i t) -> p c t i", i=LINE, t=PACK)

        widths = [sum(pieces) for pieces in PIECES]
        starts = [sum(widths[:g]) for g in range(len(PIECES))]
        last_group = len(PIECES) - 1
        used, other, third, best, hid16, banks, res, res16 = {}, {}, {}, {}, {}, {}, {}, {}

        def entries(list_tile, first, count):
            return list_tile[:, first // 16 : (first + count) // 16]

        def inside(g, j):
            first = sum(PIECES[g][:j])
            return slice(first, first + PIECES[g][j])

        def fetch(g):
            first, n = starts[g], widths[g]
            buffer = "00" if g == last_group else f"group{g}"
            used[g] = keep.tile([P, PACK, n], F32, name="used", tag=f"codes{buffer}", align_bytes=64)
            other[g] = keep.tile([P, PACK, n], F32, name="other", tag=f"plane{buffer}", align_bytes=64)
            third[g] = keep.tile([P, PACK, n], F32, name="third")
            for t in range(PACK):
                nc.scalar.activation(used[g][:, t, :], y[t][:].indirect(entries(use_t, first, n)), COPY)
                own = n
                if g == 0 and t == PACK - 1:
                    own = n - SHARE
                    nc.vector.tensor_copy(other[g][:, t, own:], y[t][:].indirect(entries(alt1_t, first + own, SHARE)))
                nc.scalar.activation(other[g][:, t, :own], y[t][:].indirect(entries(alt1_t, first, own)), COPY)
                if g > 0 and t == PACK - 1:
                    nc.scalar.activation(third[g][:, t, :], z[t][:].indirect(entries(alt2_t, first, n)), COPY)
                else:
                    nc.vector.tensor_copy(third[g][:, t, :], z[t][:].indirect(entries(alt2_t, first, n)))

        def larger(g, j):
            best[g, j] = keep.tile([P, PACK, PIECES[g][j]], F32, name=f"best{g}{j}", align_bytes=64)
            nc.vector.tensor_tensor(best[g, j][:], used[g][:, :, inside(g, j)], other[g][:, :, inside(g, j)], ALU.max)

        def round_hid(g, j):
            hid16[g, j] = keep.tile([P, PACK * PIECES[g][j]], BF16, name=f"hid16_{g}{j}", align_bytes=64)
            nc.vector.tensor_tensor(
                as_interleaved(hid16[g, j][:]), as_row_sets(best[g, j][:]), as_row_sets(third[g][:, :, inside(g, j)]), ALU.mult
            )

        def last_product(g, j):
            n = PIECES[g][j]
            codes = keep.tile([P, n], U32, name="codes", tag=f"codes{g}{j}", align_bytes=64)
            plane = keep.tile([P, n], U8, name="plane", tag=f"plane{g}{j}", align_bytes=64)
            nc.vector.quantize_mx(out=codes[:].bitcast(FP8X4), scales=plane[:], in_=hid16[g, j][:])
            banks[g, j] = [psum.tile([P, BANK], F32, name="acc") for b in range(PACK * n // BANK)]
            for t in range(PACK):
                b, at = divmod(t * n, BANK)
                product(banks[g, j][b][:, at : at + n], W3, t, codes[:], plane[:])

        def leave_psum(g, j):
            first, n = starts[g] + inside(g, j).start, PIECES[g][j]
            res[g, j] = keep.tile([P, PACK, n], F32, name=f"res_{g}{j}")
            flat = res[g, j][:].rearrange("p t n -> p (t n)")
            for b, acc in enumerate(banks[g, j]):
                nc.scalar.copy(flat[:, b * BANK : (b + 1) * BANK], acc[:])
            nc.sync.dma_start(out_rows[:, :, first : first + n], res[g, j][:])

        def round_out(g, j):
            res16[g, j] = keep.tile([P, PACK * PIECES[g][j]], BF16, name=f"res16_{g}{j}", align_bytes=64)
            copy = nc.scalar.copy if (g, j) == ROUNDED_ON_SCALAR else nc.vector.tensor_copy
            copy(as_interleaved(res16[g, j][:]), as_row_sets(res[g, j][:]))

        def hand_on(g, j):
            first, n = starts[g] + inside(g, j).start, PIECES[g][j]
            nc.vector.quantize_mx(
                out=out_codes[:, first : first + n].bitcast(FP8X4), scales=out_plane[:, first : first + n], in_=res16[g, j][:]
            )
            if j == len(PIECES[g]) - 1:
                group = slice(starts[g], starts[g] + widths[g])
                nc.sync.dma_start(out_words[:, group], out_codes[:, group].bitcast(I32))

        def stage_by_stage(stages, g):
            for stage in stages:
                for j in range(len(PIECES[g])):
                    stage(g, j)

        for g in range(len(PIECES)):
            fetch(g)
            stage_by_stage([larger, round_hid, last_product, leave_psum], g)
        for g in range(len(PIECES)):
            stage_by_stage([round_out, hand_on], g)
        for q in range(QUADRANTS):
            queue = nc.sync if q % 2 else nc.scalar
            queue.dma_start(out_2[0, 4 * q : 4 * q + 4, :].bitcast(I32), out_plane[32 * q : 32 * q + 4, :].bitcast(I32))
